import numpy as np
import ml_dtypes

BF16 = ml_dtypes.bfloat16


def bf(x):
    return np.asarray(x, np.float32).astype(BF16)


def f32(x):
    return np.asarray(x, np.float32)


def f64(x):
    return np.asarray(x).astype(np.float64)


def striped(idx):
    return np.tile(idx.reshape(-1, 16).T, (8, 1))


S, K, M, N, E, Q = 512, 128, 512, 512, 4, 128


def setup_inputs():
    return {"base": bf(np.random.standard_normal((M, S))), "x": bf(np.random.standard_normal((K, N))), "w": bf(np.random.standard_normal((E, K, M)) / np.sqrt(K)), "b": f32(0.5 * np.random.standard_normal((M, 1))), "offs": striped(np.random.permutation(S))}


def reference(base, x, w, b, offs):
    idx = offs[:16].T.reshape(-1)
    z = f64(base).copy()
    for e in range(E):
        z[:, idx[e * Q : (e + 1) * Q]] += f64(w)[e].T @ f64(x)[:, e * Q : (e + 1) * Q]
    return np.tanh(z + f64(b))

@@ -1,0 +1,62 @@
+import concourse.mybir as mybir
+from concourse.masks import make_identity
+
+BF16, F32, U16 = mybir.dt.bfloat16, mybir.dt.float32, mybir.dt.uint16
+TANH = mybir.ActivationFunctionType.Tanh
+
+P = 128
+M = 512
+S = 512
+E = 4
+Q = 128
+WINDOWS = M // P
+QCOLS = Q // 16
+
+FLOPS = 2 * P * M * E * Q
+
+
+def tile_scatter_matmul_kernel(tc, base, x, w, b, offs, out):
+    nc = tc.nc
+    with (
+        tc.tile_pool(name="held", bufs=1) as held,
+        tc.psum_pool(name="psum", bufs=1) as psum,
+    ):
+        offsets = held.tile([P, E * QCOLS], U16, name="offsets")
+        nc.sync.dma_start(offsets[:], offs)
+
+        base_blocks = []
+        for a in range(WINDOWS):
+            block = held.tile([P, S], BF16, name=f"base{a}")
+            nc.sync.dma_start(block[:], base[a * P : (a + 1) * P, :])
+            base_blocks.append(block)
+
+        x_tile = held.tile([P, E * Q], BF16, name="x_tile")
+        nc.scalar.dma_start(x_tile[:], x)
+        w_tile = held.tile([P, E, M], BF16, name="w_tile")
+        nc.scalar.dma_start(w_tile[:], w.rearrange("e k m -> k e m"))
+
+        bias = held.tile([P, WINDOWS], F32, name="bias")
+        with nc.allow_non_contiguous_dma(reason="512 single float32 values, one to a partition and window"):
+            nc.scalar.dma_start(bias[:], b.rearrange("(a p) o -> p (a o)", p=P))
+
+        ident = held.tile([P, P], BF16, name="ident")
+        make_identity(nc, ident[:])
+
+        windows = []
+        for a in range(WINDOWS):
+            window = psum.tile([P, S], F32, name=f"window{a}")
+            nc.tensor.matmul(window[:], ident[:], base_blocks[a][:], start=True, stop=False)
+            windows.append(window)
+
+        for a in range(WINDOWS):
+            for e in range(E):
+                nc.tensor.matmul(
+                    windows[a][:].indirect(offsets[:, e * QCOLS : (e + 1) * QCOLS]),
+                    w_tile[:, e, a * P : (a + 1) * P],
+                    x_tile[:, e * Q : (e + 1) * Q],
+                    start=False,
+                    stop=(e == E - 1),
+                )
+            result = held.tile([P, S], F32, name=f"result{a}")
+            nc.scalar.activation(result[:], windows[a][:], TANH, bias=bias[:, a : a + 1])
+            nc.sync.dma_start(out[a * P : (a + 1) * P, :], result[:])

@@ -12,6 +12,8 @@ Q = 128
 WINDOWS = M // P
 QCOLS = Q // 16
 
+WARM_MATMULS = 4
+
 FLOPS = 2 * P * M * E * Q
 
 
@@ -21,26 +23,42 @@ def tile_scatter_matmul_kernel(tc, base, x, w, b, offs, out):
         tc.tile_pool(name="held", bufs=1) as held,
         tc.psum_pool(name="psum", bufs=1) as psum,
     ):
-        offsets = held.tile([P, E * QCOLS], U16, name="offsets")
-        nc.sync.dma_start(offsets[:], offs)
+        queues = [nc.sync, nc.scalar]
 
         base_blocks = []
         for a in range(WINDOWS):
             block = held.tile([P, S], BF16, name=f"base{a}")
-            nc.sync.dma_start(block[:], base[a * P : (a + 1) * P, :])
+            queues[a % 2].dma_start(block[:], base[a * P : (a + 1) * P, :])
             base_blocks.append(block)
 
+        offsets = held.tile([P, E * QCOLS], U16, name="offsets")
+        nc.sync.dma_start(offsets[:], offs)
         x_tile = held.tile([P, E * Q], BF16, name="x_tile")
         nc.scalar.dma_start(x_tile[:], x)
-        w_tile = held.tile([P, E, M], BF16, name="w_tile")
-        nc.scalar.dma_start(w_tile[:], w.rearrange("e k m -> k e m"))
 
-        bias = held.tile([P, WINDOWS], F32, name="bias")
-        with nc.allow_non_contiguous_dma(reason="512 single float32 values, one to a partition and window"):
-            nc.scalar.dma_start(bias[:], b.rearrange("(a p) o -> p (a o)", p=P))
+        w_blocks = []
+        for a in range(WINDOWS):
+            w_block = held.tile([P, E, P], BF16, name=f"w{a}")
+            queues[a % 2].dma_start(w_block[:], w[:, :, a * P : (a + 1) * P].rearrange("e k m -> k e m"))
+            w_blocks.append(w_block)
 
         ident = held.tile([P, P], BF16, name="ident")
         make_identity(nc, ident[:])
+
+        bias = held.tile([P, WINDOWS], F32, name="bias")
+        with nc.allow_non_contiguous_dma(reason="512 single float32 values, one to a partition and window"):
+            nc.gpsimd.dma_start(bias[:], b.rearrange("(a p) o -> p (a o)", p=P))
+
+        zero = held.tile([P, 1], F32, name="zero")
+        nc.vector.memset(zero[:], 0.0)
+        warm = held.tile([P, 1], F32, name="warm")
+        nc.scalar.activation(warm[:], zero[:], TANH)
+
+        zeros = held.tile([P, S], BF16, name="zeros")
+        nc.vector.memset(zeros[:], 0.0)
+        idle_bank = psum.tile([P, S], F32, name="idle_bank")
+        for i in range(WARM_MATMULS):
+            nc.tensor.matmul(idle_bank[:], zeros[:, 0:P], zeros[:], start=True, stop=True)
 
         windows = []
         for a in range(WINDOWS):
@@ -52,7 +70,7 @@ def tile_scatter_matmul_kernel(tc, base, x, w, b, offs, out):
             for e in range(E):
                 nc.tensor.matmul(
                     windows[a][:].indirect(offsets[:, e * QCOLS : (e + 1) * QCOLS]),
-                    w_tile[:, e, a * P : (a + 1) * P],
+                    w_blocks[a][:, e, :],
                     x_tile[:, e * Q : (e + 1) * Q],
                     start=False,
                     stop=(e == E - 1),

@@ -10,9 +10,10 @@ S = 512
 E = 4
 Q = 128
 WINDOWS = M // P
+HALF = S // 2
 QCOLS = Q // 16
 
-WARM_MATMULS = 4
+WARM_MATMULS = 16
 
 FLOPS = 2 * P * M * E * Q
 
@@ -42,6 +43,8 @@ def tile_scatter_matmul_kernel(tc, base, x, w, b, offs, out):
             queues[a % 2].dma_start(w_block[:], w[:, :, a * P : (a + 1) * P].rearrange("e k m -> k e m"))
             w_blocks.append(w_block)
 
+        zeros = held.tile([P, P], BF16, name="zeros")
+        nc.gpsimd.memset(zeros[:], 0.0)
         ident = held.tile([P, P], BF16, name="ident")
         make_identity(nc, ident[:])
 
@@ -49,16 +52,12 @@ def tile_scatter_matmul_kernel(tc, base, x, w, b, offs, out):
         with nc.allow_non_contiguous_dma(reason="512 single float32 values, one to a partition and window"):
             nc.gpsimd.dma_start(bias[:], b.rearrange("(a p) o -> p (a o)", p=P))
 
-        zero = held.tile([P, 1], F32, name="zero")
-        nc.vector.memset(zero[:], 0.0)
         warm = held.tile([P, 1], F32, name="warm")
-        nc.scalar.activation(warm[:], zero[:], TANH)
+        nc.scalar.activation(warm[:], zeros[:, 0:1], TANH)
 
-        zeros = held.tile([P, S], BF16, name="zeros")
-        nc.vector.memset(zeros[:], 0.0)
-        idle_bank = psum.tile([P, S], F32, name="idle_bank")
+        idle_bank = psum.tile([P, P], F32, name="idle_bank")
         for i in range(WARM_MATMULS):
-            nc.tensor.matmul(idle_bank[:], zeros[:, 0:P], zeros[:], start=True, stop=True)
+            nc.tensor.matmul(idle_bank[:], zeros[:], zeros[:], start=True, stop=True)
 
         windows = []
         for a in range(WINDOWS):
@@ -75,6 +74,8 @@ def tile_scatter_matmul_kernel(tc, base, x, w, b, offs, out):
                     start=False,
                     stop=(e == E - 1),
                 )
-            result = held.tile([P, S], F32, name=f"result{a}")
-            nc.scalar.activation(result[:], windows[a][:], TANH, bias=bias[:, a : a + 1])
-            nc.sync.dma_start(out[a * P : (a + 1) * P, :], result[:])
+            for h in range(2):
+                cols = slice(h * HALF, (h + 1) * HALF)
+                result = held.tile([P, HALF], F32, name=f"result{a}_{h}")
+                nc.scalar.activation(result[:], windows[a][:, cols], TANH, bias=bias[:, a : a + 1])
+                nc.sync.dma_start(out[a * P : (a + 1) * P, cols], result[:])

@@ -10,7 +10,6 @@ S = 512
 E = 4
 Q = 128
 WINDOWS = M // P
-HALF = S // 2
 QCOLS = Q // 16
 
 WARM_MATMULS = 16
@@ -37,6 +36,10 @@ def tile_scatter_matmul_kernel(tc, base, x, w, b, offs, out):
         x_tile = held.tile([P, E * Q], BF16, name="x_tile")
         nc.scalar.dma_start(x_tile[:], x)
 
+        bias = held.tile([P, WINDOWS], F32, name="bias")
+        with nc.allow_non_contiguous_dma(reason="512 single float32 values, one to a partition and window"):
+            nc.scalar.dma_start(bias[:], b.rearrange("(a p) o -> p (a o)", p=P))
+
         w_blocks = []
         for a in range(WINDOWS):
             w_block = held.tile([P, E, P], BF16, name=f"w{a}")
@@ -47,10 +50,6 @@ def tile_scatter_matmul_kernel(tc, base, x, w, b, offs, out):
         nc.gpsimd.memset(zeros[:], 0.0)
         ident = held.tile([P, P], BF16, name="ident")
         make_identity(nc, ident[:])
-
-        bias = held.tile([P, WINDOWS], F32, name="bias")
-        with nc.allow_non_contiguous_dma(reason="512 single float32 values, one to a partition and window"):
-            nc.gpsimd.dma_start(bias[:], b.rearrange("(a p) o -> p (a o)", p=P))
 
         warm = held.tile([P, 1], F32, name="warm")
         nc.scalar.activation(warm[:], zeros[:, 0:1], TANH)
@@ -74,8 +73,6 @@ def tile_scatter_matmul_kernel(tc, base, x, w, b, offs, out):
                     start=False,
                     stop=(e == E - 1),
                 )
-            for h in range(2):
-                cols = slice(h * HALF, (h + 1) * HALF)
-                result = held.tile([P, HALF], F32, name=f"result{a}_{h}")
-                nc.scalar.activation(result[:], windows[a][:, cols], TANH, bias=bias[:, a : a + 1])
-                nc.sync.dma_start(out[a * P : (a + 1) * P, cols], result[:])
+            result = held.tile([P, S], F32, name=f"result{a}")
+            nc.scalar.activation(result[:], windows[a][:], TANH, bias=bias[:, a : a + 1])
+            nc.sync.dma_start(out[a * P : (a + 1) * P, :], result[:])

@@ -23,28 +23,27 @@ def tile_scatter_matmul_kernel(tc, base, x, w, b, offs, out):
         tc.tile_pool(name="held", bufs=1) as held,
         tc.psum_pool(name="psum", bufs=1) as psum,
     ):
-        queues = [nc.sync, nc.scalar]
 
-        base_blocks = []
-        for a in range(WINDOWS):
-            block = held.tile([P, S], BF16, name=f"base{a}")
-            queues[a % 2].dma_start(block[:], base[a * P : (a + 1) * P, :])
-            base_blocks.append(block)
+        base_pairs = []
+        for h in range(WINDOWS // 2):
+            pair = held.tile([P, 2, S], BF16, name=f"base_pair{h}")
+            nc.sync.dma_start(pair[:], base[2 * h * P : (2 * h + 2) * P, :].rearrange("(i p) s -> p i s", p=P))
+            base_pairs.append(pair)
 
         offsets = held.tile([P, E * QCOLS], U16, name="offsets")
         nc.sync.dma_start(offsets[:], offs)
         x_tile = held.tile([P, E * Q], BF16, name="x_tile")
-        nc.scalar.dma_start(x_tile[:], x)
+        nc.sync.dma_start(x_tile[:], x)
+
+        w_pairs = []
+        for h in range(WINDOWS // 2):
+            w_pair = held.tile([P, E, 2 * P], BF16, name=f"w_pair{h}")
+            nc.sync.dma_start(w_pair[:], w[:, :, 2 * h * P : (2 * h + 2) * P].rearrange("e k m -> k e m"))
+            w_pairs.append(w_pair)
 
         bias = held.tile([P, WINDOWS], F32, name="bias")
         with nc.allow_non_contiguous_dma(reason="512 single float32 values, one to a partition and window"):
-            nc.scalar.dma_start(bias[:], b.rearrange("(a p) o -> p (a o)", p=P))
-
-        w_blocks = []
-        for a in range(WINDOWS):
-            w_block = held.tile([P, E, P], BF16, name=f"w{a}")
-            queues[a % 2].dma_start(w_block[:], w[:, :, a * P : (a + 1) * P].rearrange("e k m -> k e m"))
-            w_blocks.append(w_block)
+            nc.sync.dma_start(bias[:], b.rearrange("(a p) o -> p (a o)", p=P))
 
         zeros = held.tile([P, P], BF16, name="zeros")
         nc.gpsimd.memset(zeros[:], 0.0)
@@ -61,14 +60,14 @@ def tile_scatter_matmul_kernel(tc, base, x, w, b, offs, out):
         windows = []
         for a in range(WINDOWS):
             window = psum.tile([P, S], F32, name=f"window{a}")
-            nc.tensor.matmul(window[:], ident[:], base_blocks[a][:], start=True, stop=False)
+            nc.tensor.matmul(window[:], ident[:], base_pairs[a // 2][:, a % 2, :], start=True, stop=False)
             windows.append(window)
 
         for a in range(WINDOWS):
             for e in range(E):
                 nc.tensor.matmul(
                     windows[a][:].indirect(offsets[:, e * QCOLS : (e + 1) * QCOLS]),
-                    w_blocks[a][:, e, :],
+                    w_pairs[a // 2][:, e, (a % 2) * P : (a % 2 + 1) * P],
                     x_tile[:, e * Q : (e + 1) * Q],
                     start=False,
                     stop=(e == E - 1),

@@ -35,11 +35,11 @@ def tile_scatter_matmul_kernel(tc, base, x, w, b, offs, out):
         x_tile = held.tile([P, E * Q], BF16, name="x_tile")
         nc.sync.dma_start(x_tile[:], x)
 
-        w_pairs = []
-        for h in range(WINDOWS // 2):
-            w_pair = held.tile([P, E, 2 * P], BF16, name=f"w_pair{h}")
-            nc.sync.dma_start(w_pair[:], w[:, :, 2 * h * P : (2 * h + 2) * P].rearrange("e k m -> k e m"))
-            w_pairs.append(w_pair)
+        w_blocks = []
+        for a in range(WINDOWS):
+            w_block = held.tile([P, E, P], BF16, name=f"w{a}")
+            nc.sync.dma_start(w_block[:], w[:, :, a * P : (a + 1) * P].rearrange("e k m -> k e m"))
+            w_blocks.append(w_block)
 
         bias = held.tile([P, WINDOWS], F32, name="bias")
         with nc.allow_non_contiguous_dma(reason="512 single float32 values, one to a partition and window"):
@@ -67,7 +67,7 @@ def tile_scatter_matmul_kernel(tc, base, x, w, b, offs, out):
             for e in range(E):
                 nc.tensor.matmul(
                     windows[a][:].indirect(offsets[:, e * QCOLS : (e + 1) * QCOLS]),
-                    w_pairs[a // 2][:, e, (a % 2) * P : (a % 2 + 1) * P],
+                    w_blocks[a][:, e, :],
                     x_tile[:, e * Q : (e + 1) * Q],
                     start=False,
                     stop=(e == E - 1),

@@ -35,15 +35,15 @@ def tile_scatter_matmul_kernel(tc, base, x, w, b, offs, out):
         x_tile = held.tile([P, E * Q], BF16, name="x_tile")
         nc.sync.dma_start(x_tile[:], x)
 
+        bias = held.tile([P, WINDOWS], F32, name="bias")
         w_blocks = []
         for a in range(WINDOWS):
             w_block = held.tile([P, E, P], BF16, name=f"w{a}")
             nc.sync.dma_start(w_block[:], w[:, :, a * P : (a + 1) * P].rearrange("e k m -> k e m"))
             w_blocks.append(w_block)
-
-        bias = held.tile([P, WINDOWS], F32, name="bias")
-        with nc.allow_non_contiguous_dma(reason="512 single float32 values, one to a partition and window"):
-            nc.sync.dma_start(bias[:], b.rearrange("(a p) o -> p (a o)", p=P))
+            if a == 0:
+                with nc.allow_non_contiguous_dma(reason="512 single float32 values, one to a partition and window"):
+                    nc.sync.dma_start(bias[:], b.rearrange("(a p) o -> p (a o)", p=P))
 
         zeros = held.tile([P, P], BF16, name="zeros")
         nc.gpsimd.memset(zeros[:], 0.0)

@@ -24,11 +24,11 @@ def tile_scatter_matmul_kernel(tc, base, x, w, b, offs, out):
         tc.psum_pool(name="psum", bufs=1) as psum,
     ):
 
-        base_pairs = []
-        for h in range(WINDOWS // 2):
-            pair = held.tile([P, 2, S], BF16, name=f"base_pair{h}")
-            nc.sync.dma_start(pair[:], base[2 * h * P : (2 * h + 2) * P, :].rearrange("(i p) s -> p i s", p=P))
-            base_pairs.append(pair)
+        base_blocks = []
+        for a in range(WINDOWS):
+            block = held.tile([P, S], BF16, name=f"base{a}")
+            nc.sync.dma_start(block[:], base[a * P : (a + 1) * P, :])
+            base_blocks.append(block)
 
         offsets = held.tile([P, E * QCOLS], U16, name="offsets")
         nc.sync.dma_start(offsets[:], offs)
@@ -60,7 +60,7 @@ def tile_scatter_matmul_kernel(tc, base, x, w, b, offs, out):
         windows = []
         for a in range(WINDOWS):
             window = psum.tile([P, S], F32, name=f"window{a}")
-            nc.tensor.matmul(window[:], ident[:], base_pairs[a // 2][:, a % 2, :], start=True, stop=False)
+            nc.tensor.matmul(window[:], ident[:], base_blocks[a][:], start=True, stop=False)
             windows.append(window)
 
         for a in range(WINDOWS):

@@ -41,7 +41,7 @@ def tile_scatter_matmul_kernel(tc, base, x, w, b, offs, out):
             w_block = held.tile([P, E, P], BF16, name=f"w{a}")
             nc.sync.dma_start(w_block[:], w[:, :, a * P : (a + 1) * P].rearrange("e k m -> k e m"))
             w_blocks.append(w_block)
-            if a == 0:
+            if a == 1:
                 with nc.allow_non_contiguous_dma(reason="512 single float32 values, one to a partition and window"):
                     nc.sync.dma_start(bias[:], b.rearrange("(a p) o -> p (a o)", p=P))
 

@@ -72,6 +72,9 @@ def tile_scatter_matmul_kernel(tc, base, x, w, b, offs, out):
                     start=False,
                     stop=(e == E - 1),
                 )
-            result = held.tile([P, S], F32, name=f"result{a}")
-            nc.scalar.activation(result[:], windows[a][:], TANH, bias=bias[:, a : a + 1])
-            nc.sync.dma_start(out[a * P : (a + 1) * P, :], result[:])
+            halves = 2 if a == WINDOWS - 1 else 1
+            width = S // halves
+            for h in range(halves):
+                result = held.tile([P, width], F32, name=f"result{a}_{h}")
+                nc.scalar.activation(result[:], windows[a][:, h * width : (h + 1) * width], TANH, bias=bias[:, a : a + 1])
+                nc.sync.dma_start(out[a * P : (a + 1) * P, h * width : (h + 1) * width], result[:])

@@ -12,7 +12,7 @@ Q = 128
 WINDOWS = M // P
 QCOLS = Q // 16
 
-WARM_MATMULS = 16
+WARM_MATMULS = 8
 
 FLOPS = 2 * P * M * E * Q
 

@@ -35,20 +35,22 @@ def tile_scatter_matmul_kernel(tc, base, x, w, b, offs, out):
         x_tile = held.tile([P, E * Q], BF16, name="x_tile")
         nc.sync.dma_start(x_tile[:], x)
 
-        bias = held.tile([P, WINDOWS], F32, name="bias")
         w_blocks = []
         for a in range(WINDOWS):
             w_block = held.tile([P, E, P], BF16, name=f"w{a}")
             nc.sync.dma_start(w_block[:], w[:, :, a * P : (a + 1) * P].rearrange("e k m -> k e m"))
             w_blocks.append(w_block)
-            if a == 1:
-                with nc.allow_non_contiguous_dma(reason="512 single float32 values, one to a partition and window"):
-                    nc.sync.dma_start(bias[:], b.rearrange("(a p) o -> p (a o)", p=P))
+
+        bias_rows = held.tile([P, P], F32, name="bias_rows")
+        nc.vector.memset(bias_rows[:], 0.0)
+        nc.scalar.dma_start(bias_rows[0:WINDOWS, :], b.rearrange("(a p) o -> a (p o)", p=P))
 
         zeros = held.tile([P, P], BF16, name="zeros")
         nc.gpsimd.memset(zeros[:], 0.0)
         ident = held.tile([P, P], BF16, name="ident")
         make_identity(nc, ident[:])
+        ident_f32 = held.tile([P, P], F32, name="ident_f32")
+        make_identity(nc, ident_f32[:])
 
         warm = held.tile([P, 1], F32, name="warm")
         nc.scalar.activation(warm[:], zeros[:, 0:1], TANH)
@@ -62,6 +64,11 @@ def tile_scatter_matmul_kernel(tc, base, x, w, b, offs, out):
             window = psum.tile([P, S], F32, name=f"window{a}")
             nc.tensor.matmul(window[:], ident[:], base_blocks[a][:], start=True, stop=False)
             windows.append(window)
+
+        bias_bank = psum.tile([P, P], F32, name="bias_bank")
+        nc.tensor.transpose(bias_bank[:], bias_rows[:], ident_f32[:])
+        bias = held.tile([P, WINDOWS], F32, name="bias")
+        nc.vector.tensor_copy(bias[:], bias_bank[:, 0:WINDOWS])
 
         for a in range(WINDOWS):
             for e in range(E):

@@ -36,10 +36,11 @@ def tile_scatter_matmul_kernel(tc, base, x, w, b, offs, out):
         nc.sync.dma_start(x_tile[:], x)
 
         w_blocks = []
-        for a in range(WINDOWS):
-            w_block = held.tile([P, E, P], BF16, name=f"w{a}")
-            nc.sync.dma_start(w_block[:], w[:, :, a * P : (a + 1) * P].rearrange("e k m -> k e m"))
-            w_blocks.append(w_block)
+        for first, count in ((0, 1), (1, 1), (2, 2)):
+            w_part = held.tile([P, E, count * P], BF16, name=f"w{first}")
+            nc.sync.dma_start(w_part[:], w[:, :, first * P : (first + count) * P].rearrange("e k m -> k e m"))
+            for i in range(count):
+                w_blocks.append([w_part[:, e, i * P : (i + 1) * P] for e in range(E)])
 
         bias_rows = held.tile([P, P], F32, name="bias_rows")
         nc.vector.memset(bias_rows[:], 0.0)
@@ -74,7 +75,7 @@ def tile_scatter_matmul_kernel(tc, base, x, w, b, offs, out):
             for e in range(E):
                 nc.tensor.matmul(
                     windows[a][:].indirect(offsets[:, e * QCOLS : (e + 1) * QCOLS]),
-                    w_blocks[a][:, e, :],
+                    w_blocks[a][e],
                     x_tile[:, e * Q : (e + 1) * Q],
                     start=False,
                     stop=(e == E - 1),

@@ -80,7 +80,7 @@ def tile_scatter_matmul_kernel(tc, base, x, w, b, offs, out):
                     start=False,
                     stop=(e == E - 1),
                 )
-            halves = 2 if a == WINDOWS - 1 else 1
+            halves = 2 if a >= WINDOWS - 2 else 1
             width = S // halves
             for h in range(halves):
                 result = held.tile([P, width], F32, name=f"result{a}_{h}")

import concourse.mybir as mybir
from concourse.masks import make_identity

BF16, F32, U16 = mybir.dt.bfloat16, mybir.dt.float32, mybir.dt.uint16
TANH = mybir.ActivationFunctionType.Tanh

P = 128
M = 512
S = 512
E = 4
Q = 128
WINDOWS = M // P
QCOLS = Q // 16

WARM_MATMULS = 8

FLOPS = 2 * P * M * E * Q


def tile_scatter_matmul_kernel(tc, base, x, w, b, offs, out):
    nc = tc.nc
    with (
        tc.tile_pool(name="held", bufs=1) as held,
        tc.psum_pool(name="psum", bufs=1) as psum,
    ):

        base_blocks = []
        for a in range(WINDOWS):
            block = held.tile([P, S], BF16, name=f"base{a}")
            nc.sync.dma_start(block[:], base[a * P : (a + 1) * P, :])
            base_blocks.append(block)

        offsets = held.tile([P, E * QCOLS], U16, name="offsets")
        nc.sync.dma_start(offsets[:], offs)
        x_tile = held.tile([P, E * Q], BF16, name="x_tile")
        nc.sync.dma_start(x_tile[:], x)

        w_blocks = []
        for first, count in ((0, 1), (1, 1), (2, 2)):
            w_part = held.tile([P, E, count * P], BF16, name=f"w{first}")
            nc.sync.dma_start(w_part[:], w[:, :, first * P : (first + count) * P].rearrange("e k m -> k e m"))
            for i in range(count):
                w_blocks.append([w_part[:, e, i * P : (i + 1) * P] for e in range(E)])

        bias_rows = held.tile([P, P], F32, name="bias_rows")
        nc.vector.memset(bias_rows[:], 0.0)
        nc.scalar.dma_start(bias_rows[0:WINDOWS, :], b.rearrange("(a p) o -> a (p o)", p=P))

        zeros = held.tile([P, P], BF16, name="zeros")
        nc.gpsimd.memset(zeros[:], 0.0)
        ident = held.tile([P, P], BF16, name="ident")
        make_identity(nc, ident[:])
        ident_f32 = held.tile([P, P], F32, name="ident_f32")
        make_identity(nc, ident_f32[:])

        warm = held.tile([P, 1], F32, name="warm")
        nc.scalar.activation(warm[:], zeros[:, 0:1], TANH)

        idle_bank = psum.tile([P, P], F32, name="idle_bank")
        for i in range(WARM_MATMULS):
            nc.tensor.matmul(idle_bank[:], zeros[:], zeros[:], start=True, stop=True)

        windows = []
        for a in range(WINDOWS):
            window = psum.tile([P, S], F32, name=f"window{a}")
            nc.tensor.matmul(window[:], ident[:], base_blocks[a][:], start=True, stop=False)
            windows.append(window)

        bias_bank = psum.tile([P, P], F32, name="bias_bank")
        nc.tensor.transpose(bias_bank[:], bias_rows[:], ident_f32[:])
        bias = held.tile([P, WINDOWS], F32, name="bias")
        nc.vector.tensor_copy(bias[:], bias_bank[:, 0:WINDOWS])

        for a in range(WINDOWS):
            for e in range(E):
                nc.tensor.matmul(
                    windows[a][:].indirect(offsets[:, e * QCOLS : (e + 1) * QCOLS]),
                    w_blocks[a][e],
                    x_tile[:, e * Q : (e + 1) * Q],
                    start=False,
                    stop=(e == E - 1),
                )
            halves = 2 if a >= WINDOWS - 2 else 1
            width = S // halves
            for h in range(halves):
                result = held.tile([P, width], F32, name=f"result{a}_{h}")
                nc.scalar.activation(result[:], windows[a][:, h * width : (h + 1) * width], TANH, bias=bias[:, a : a + 1])
                nc.sync.dma_start(out[a * P : (a + 1) * P, h * width : (h + 1) * width], result[:])
